import numpy as np
import ml_dtypes


def mxq(x, axis, fmt="e4m3"):
    dtype, down = {"e4m3": (ml_dtypes.float8_e4m3fn, 7), "e5m2": (ml_dtypes.float8_e5m2, 14)}[fmt]
    v = np.moveaxis(np.asarray(x, np.float32).astype(ml_dtypes.bfloat16).astype(np.float64), axis, -1)
    blocks = v.reshape(v.shape[:-1] + (-1, 32))
    amax = np.abs(blocks).max(-1, keepdims=True)
    byte = np.maximum(np.where(amax > 0, np.frexp(amax)[1] - 1 + 127, 0) - down, 1)
    scale = np.exp2(byte - 127.0)
    codes = (blocks / scale).astype(np.float32).astype(dtype).astype(np.float64)
    return np.moveaxis((codes * scale).reshape(v.shape), -1, axis)


WIDE = False


def mx_kscale(k):
    if not WIDE:
        return np.ones(k)
    levels = np.array([10, -10, 5, -5, 0])
    if k % 512:
        return np.exp2(np.random.permutation(np.resize(levels, k // 32))).repeat(32)
    a = np.empty((k // 512, 16))
    for p in range(k // 512):
        a[p, :8] = np.random.permutation(np.resize(levels, 8))
        for g in range(8):
            far = levels[np.abs(levels - a[p, g]) >= 10]
            a[p, g + 8] = far[np.random.randint(len(far))]
    return np.exp2(a.ravel()).repeat(32)


def f64(x):
    return np.asarray(x).astype(np.float64)


def striped(idx):
    return np.tile(idx.reshape(-1, 16).T, (8, 1)).astype(np.uint16)


def unstriped(offs):
    return offs[:16].T.reshape(-1).astype(np.int64)


def pack_weight(w):
    k, n = w.shape
    w = f64(np.asarray(w, np.float32).astype(ml_dtypes.bfloat16)).reshape(k // 32, 32, n)
    amax = np.abs(w).max(1)
    byte = np.clip(np.where(amax > 0, np.frexp(amax)[1] - 1 + 127 - 7, 1), 1, 254)
    scaled = (w * np.exp2(127.0 - byte)[:, None, :]).reshape(k, n).astype(np.float32)
    words = np.ascontiguousarray(scaled.reshape(k // 512, 128, 4, n).transpose(0, 1, 3, 2)).astype(ml_dtypes.float8_e4m3fn).view(np.uint8)
    return words, np.ascontiguousarray(byte.astype(np.uint8).reshape(k // 512, 16, n))


def unpack_weight(words, scales):
    g, p, n, _ = words.shape
    vals = np.ascontiguousarray(words).view(ml_dtypes.float8_e4m3fn).astype(np.float64) * np.repeat(np.exp2(scales.astype(np.float64) - 127.0), 8, axis=1)[..., None]
    return vals.transpose(0, 1, 3, 2).reshape(g * 512, n)


K, T, S, J = 1024, 2048, 512, 256


def setup_inputs():
    n = np.random.standard_normal
    s = mx_kscale(K)[:, None]
    part = np.random.uniform(0.2, 0.8, (J, 1))
    packed_xT = pack_weight(n((K, T)) * s)
    return {
        "x_words": packed_xT[0],
        "x_scales": packed_xT[1],
        "hT": (n((K, J)) / np.sqrt(K) / s).astype(np.float32),
        "gT": (n((K, J)) / np.sqrt(K) / s).astype(np.float32),
        "mix": (np.concatenate([part, 1.0 - part], axis=1)).astype(np.float32),
        "offs": striped(np.random.permutation(T)[:S]),
    }


def reference(x_words, x_scales, hT, gT, mix, offs):
    hTq = mxq(f64(hT), 0, "e4m3")
    xq = unpack_weight(x_words, x_scales)[:, unstriped(offs)]
    y = hTq.T @ xq
    e = np.exp(y - y.max(axis=1, keepdims=True))
    p = e / e.sum(axis=1, keepdims=True)
    gTq = mxq(f64(gT), 0, "e4m3")
    z = gTq.T @ xq
    e = np.exp(z - z.max(axis=1, keepdims=True))
    q = e / e.sum(axis=1, keepdims=True)
    return f64(mix)[:, 0:1] * p + f64(mix)[:, 1:2] * q

@@ -1,0 +1,144 @@
+from contextlib import ExitStack
+
+import concourse.mybir as mybir
+
+K, T, S, J = 1024, 2048, 512, 256
+FLOPS = 2 * 2 * K * J * S
+
+F32 = mybir.dt.float32
+BF16 = mybir.dt.bfloat16
+I32 = mybir.dt.int32
+U32 = mybir.dt.uint32
+U16 = mybir.dt.uint16
+U8 = mybir.dt.uint8
+FP8X4 = mybir.dt.float8_e4m3fn_x4
+ALU = mybir.AluOpType
+ACT = mybir.ActivationFunctionType
+AX = mybir.AxisListType
+
+P = 128
+PACK = 4
+K_PASS = P * PACK
+PASSES = K // K_PASS
+TILES = J // P
+
+
+def tile_picked_zmos_soft_p_kernel(tc, x_words, x_scales, hT, gT, mix, offs, out):
+    nc = tc.nc
+    with ExitStack() as ctx:
+        keep = ctx.enter_context(tc.tile_pool(name="keep", bufs=1))
+        psum = ctx.enter_context(tc.psum_pool(name="psum", bufs=1))
+
+        offsets = keep.tile([P, S // 16], U16, name="offsets")
+        words = [keep.tile([P, T], U32, name="words%d" % o, align_bytes=64) for o in range(PASSES)]
+        planes = keep.tile([P, T], U8, name="planes", align_bytes=64)
+        raw = {(m, o): keep.tile([P, PACK, J], F32, name="raw%d%d" % (m, o), align_bytes=64) for m in range(2) for o in range(PASSES)}
+        weights = keep.tile([P, TILES, 2], F32, name="weights")
+        warm_in = keep.tile([P, 1], F32, name="warm_in")
+        warm_out = keep.tile([P, 1], F32, name="warm_out")
+
+        nc.vector.memset(planes[:].bitcast(I32), 0)
+        nc.vector.memset(warm_in[:], 0.0)
+        nc.scalar.activation(out=warm_out[:], in_=warm_in[:], func=ACT.Exp)
+
+        def load_words(o):
+            nc.sync.dma_start(out=words[o][:].bitcast(I32), in_=x_words[o].rearrange("p n r -> p (n r)").bitcast(I32))
+
+        def load_context(m, o):
+            rows = (hT, gT)[m][o * K_PASS : (o + 1) * K_PASS, :]
+            nc.sync.dma_start(out=raw[m, o][:], in_=rows.rearrange("(p j) c -> p j c", j=PACK))
+
+        load_words(0)
+        nc.sync.dma_start(offsets[:], offs)
+        for q in range(4):
+            nc.sync.dma_start(out=planes[32 * q : 32 * q + 8, :].bitcast(I32), in_=x_scales[:, 4 * q : 4 * q + 4, :].bitcast(I32))
+        load_context(0, 0)
+        load_words(1)
+        load_context(0, 1)
+        load_context(1, 0)
+        load_context(1, 1)
+        nc.sync.dma_start(out=weights[:], in_=mix.rearrange("(t p) c -> p t c", p=P))
+
+        picked_planes = keep.tile([P, S], U8, name="picked_planes", align_bytes=64)
+        picked = [keep.tile([P, S], U32, name="picked%d" % o, align_bytes=64) for o in range(PASSES)]
+        banks = {(m, t): psum.tile([P, S], F32, name="bank%d%d" % (m, t)) for m in range(2) for t in range(TILES)}
+
+        def gather_words(o):
+            nc.vector.tensor_copy(picked[o][:], words[o][:].indirect(offsets[:]))
+
+        grouped = {}
+
+        def interleave(m, o, t, on_vector):
+            dst = keep.tile([P, P, PACK], BF16, name="grouped%d%d%d" % (m, o, t), align_bytes=64)
+            grouped[m, o, t] = dst
+            dst_view = dst[:].rearrange("p (c i) j -> p c j i", i=4)
+            src_view = raw[m, o][:, :, t * P : (t + 1) * P].rearrange("p j (c i) -> p c j i", i=4)
+            if on_vector:
+                nc.vector.tensor_copy(out=dst_view, in_=src_view)
+            else:
+                nc.scalar.copy(out=dst_view, in_=src_view)
+
+        def multiply(m, o, t):
+            codes = keep.tile([P, P], U32, name="codes%d%d%d" % (m, o, t), align_bytes=64)
+            scales = keep.tile([P, P], U8, name="scales%d%d%d" % (m, o, t), align_bytes=64)
+            nc.vector.quantize_mx(out=codes[:].bitcast(FP8X4), scales=scales[:], in_=grouped[m, o, t][:].rearrange("p c j -> p (c j)"))
+            nc.tensor.matmul_mx(
+                out=banks[m, t][:],
+                lhsT=codes[:].bitcast(FP8X4),
+                lhsT_scale=scales[:],
+                rhs=picked[o][:].bitcast(FP8X4),
+                rhs_scale=picked_planes[4 * o : P, :],
+                start=(o == 0),
+                stop=(o == PASSES - 1),
+            )
+
+        exps = {}
+        inverse = {}
+
+        totals = {}
+        first = {}
+
+        def exponentiate(m, t):
+            neg_max = keep.tile([P, 1], F32, name="neg_max%d%d" % (m, t))
+            totals[m, t] = keep.tile([P, 1], F32, name="total%d%d" % (m, t))
+            exps[m, t] = keep.tile([P, S], F32, name="exps%d%d" % (m, t))
+            nc.vector.tensor_reduce(out=neg_max[:], in_=banks[m, t][:], axis=AX.X, op=ALU.max, negate=True)
+            nc.scalar.activation(out=exps[m, t][:], in_=banks[m, t][:], func=ACT.Exp, bias=neg_max[:], scale=1.0, accum_out=totals[m, t][:])
+
+        def invert(m, t):
+            inverse[m, t] = keep.tile([P, 1], F32, name="inverse%d%d" % (m, t))
+            nc.vector.reciprocal(out=inverse[m, t][:], in_=totals[m, t][:])
+
+        def weigh_first(t):
+            invert(0, t)
+            first[t] = keep.tile([P, S], F32, name="first%d" % t)
+            nc.vector.tensor_scalar(out=first[t][:], in0=exps[0, t][:], scalar1=inverse[0, t][:], scalar2=weights[:, t, 0:1], op0=ALU.mult, op1=ALU.mult)
+
+        def finish(t):
+            invert(1, t)
+            factor = keep.tile([P, 1], F32, name="factor%d" % t)
+            result = keep.tile([P, S], F32, name="result%d" % t)
+            nc.vector.tensor_tensor(out=factor[:], in0=inverse[1, t][:], in1=weights[:, t, 1:2], op=ALU.mult)
+            nc.vector.scalar_tensor_tensor(out=result[:], in0=exps[1, t][:], scalar=factor[:], in1=first[t][:], op0=ALU.mult, op1=ALU.add)
+            nc.sync.dma_start(out=out[t * P : (t + 1) * P, :], in_=result[:])
+
+        gather_words(0)
+        nc.vector.tensor_copy(picked_planes[:], planes[:].indirect(offsets[:]))
+        for t in range(TILES):
+            interleave(0, 0, t, False)
+        for t in range(TILES):
+            multiply(0, 0, t)
+        gather_words(1)
+        for m, o in ((0, 1), (1, 0), (1, 1)):
+            for t in range(TILES):
+                interleave(m, o, t, t == 0)
+            for t in range(TILES):
+                multiply(m, o, t)
+        exponentiate(0, 0)
+        exponentiate(0, 1)
+        exponentiate(1, 0)
+        exponentiate(1, 1)
+        weigh_first(0)
+        finish(0)
+        weigh_first(1)
+        finish(1)

@@ -94,16 +94,24 @@ def tile_picked_zmos_soft_p_kernel(tc, x_words, x_scales, hT, gT, mix, offs, out
 
         exps = {}
         inverse = {}
-
         totals = {}
         first = {}
 
+        def runs(ap):
+            return ap.rearrange("p (j c) -> p j c", j=PACK)
+
         def exponentiate(m, t):
-            neg_max = keep.tile([P, 1], F32, name="neg_max%d%d" % (m, t))
+            if (m, t) == (0, 1):
+                neg_max = grouped[1, 1, 1][:].rearrange("p c j -> p (c j)").bitcast(F32)[:, 0:1]
+            else:
+                neg_max = keep.tile([P, 1], F32, name="neg_max%d%d" % (m, t))[:]
             totals[m, t] = keep.tile([P, 1], F32, name="total%d%d" % (m, t))
-            exps[m, t] = keep.tile([P, S], F32, name="exps%d%d" % (m, t))
-            nc.vector.tensor_reduce(out=neg_max[:], in_=banks[m, t][:], axis=AX.X, op=ALU.max, negate=True)
-            nc.scalar.activation(out=exps[m, t][:], in_=banks[m, t][:], func=ACT.Exp, bias=neg_max[:], scale=1.0, accum_out=totals[m, t][:])
+            if (m, t) == (0, 0):
+                exps[m, t] = raw[1, 1][:, :, P : 2 * P]
+            else:
+                exps[m, t] = runs(keep.tile([P, S], F32, name="exps%d%d" % (m, t))[:])
+            nc.vector.tensor_reduce(out=neg_max, in_=banks[m, t][:], axis=AX.X, op=ALU.max, negate=True)
+            nc.scalar.activation(out=exps[m, t], in_=runs(banks[m, t][:]), func=ACT.Exp, bias=neg_max, scale=1.0, accum_out=totals[m, t][:])
 
         def invert(m, t):
             inverse[m, t] = keep.tile([P, 1], F32, name="inverse%d%d" % (m, t))
@@ -112,15 +120,22 @@ def tile_picked_zmos_soft_p_kernel(tc, x_words, x_scales, hT, gT, mix, offs, out
         def weigh_first(t):
             invert(0, t)
             first[t] = keep.tile([P, S], F32, name="first%d" % t)
-            nc.vector.tensor_scalar(out=first[t][:], in0=exps[0, t][:], scalar1=inverse[0, t][:], scalar2=weights[:, t, 0:1], op0=ALU.mult, op1=ALU.mult)
+            nc.vector.tensor_scalar(out=runs(first[t][:]), in0=exps[0, t], scalar1=inverse[0, t][:], scalar2=weights[:, t, 0:1], op0=ALU.mult, op1=ALU.mult)
+
+        factor = {}
+
+        def weigh_second(t):
+            invert(1, t)
+            factor[t] = keep.tile([P, 1], F32, name="factor%d" % t)
+            nc.vector.tensor_tensor(out=factor[t][:], in0=inverse[1, t][:], in1=weights[:, t, 1:2], op=ALU.mult)
 
         def finish(t):
-            invert(1, t)
-            factor = keep.tile([P, 1], F32, name="factor%d" % t)
-            result = keep.tile([P, S], F32, name="result%d" % t)
-            nc.vector.tensor_tensor(out=factor[:], in0=inverse[1, t][:], in1=weights[:, t, 1:2], op=ALU.mult)
-            nc.vector.scalar_tensor_tensor(out=result[:], in0=exps[1, t][:], scalar=factor[:], in1=first[t][:], op0=ALU.mult, op1=ALU.add)
-            nc.sync.dma_start(out=out[t * P : (t + 1) * P, :], in_=result[:])
+            for u, queue in enumerate((nc.sync, nc.scalar)):
+                half = keep.tile([P, S // 2], F32, name="result%d%d" % (t, u))
+                cols = slice(u * S // 2, (u + 1) * S // 2)
+                second = exps[1, t].rearrange("p j c -> p (j c)")
+                nc.vector.scalar_tensor_tensor(out=half[:], in0=second[:, cols], scalar=factor[t][:], in1=first[t][:, cols], op0=ALU.mult, op1=ALU.add)
+                queue.dma_start(out=out[t * P : (t + 1) * P, cols], in_=half[:])
 
         gather_words(0)
         nc.vector.tensor_copy(picked_planes[:], planes[:].indirect(offsets[:]))
@@ -138,7 +153,9 @@ def tile_picked_zmos_soft_p_kernel(tc, x_words, x_scales, hT, gT, mix, offs, out
         exponentiate(0, 1)
         exponentiate(1, 0)
         exponentiate(1, 1)
-        weigh_first(0)
-        finish(0)
-        weigh_first(1)
-        finish(1)
+        for t in range(TILES):
+            weigh_second(t)
+        for t in range(TILES):
+            weigh_first(t)
+        for t in range(TILES):
+            finish(t)

@@ -32,7 +32,7 @@ def tile_picked_zmos_soft_p_kernel(tc, x_words, x_scales, hT, gT, mix, offs, out
         offsets = keep.tile([P, S // 16], U16, name="offsets")
         words = [keep.tile([P, T], U32, name="words%d" % o, align_bytes=64) for o in range(PASSES)]
         planes = keep.tile([P, T], U8, name="planes", align_bytes=64)
-        raw = {(m, o): keep.tile([P, PACK, J], F32, name="raw%d%d" % (m, o), align_bytes=64) for m in range(2) for o in range(PASSES)}
+        raw = {(m, o): keep.tile([P, PACK + 1, J], F32, name="raw%d%d" % (m, o), align_bytes=64) for m in range(2) for o in range(PASSES)}
         weights = keep.tile([P, TILES, 2], F32, name="weights")
         warm_in = keep.tile([P, 1], F32, name="warm_in")
         warm_out = keep.tile([P, 1], F32, name="warm_out")
@@ -46,11 +46,11 @@ def tile_picked_zmos_soft_p_kernel(tc, x_words, x_scales, hT, gT, mix, offs, out
 
         def load_context(m, o):
             rows = (hT, gT)[m][o * K_PASS : (o + 1) * K_PASS, :]
-            nc.sync.dma_start(out=raw[m, o][:], in_=rows.rearrange("(p j) c -> p j c", j=PACK))
+            nc.sync.dma_start(out=raw[m, o][:, 0:PACK, :], in_=rows.rearrange("(p j) c -> p j c", j=PACK))
 
         load_words(0)
         nc.sync.dma_start(offsets[:], offs)
-        for q in range(4):
+        for q in (0, 2, 1, 3):
             nc.sync.dma_start(out=planes[32 * q : 32 * q + 8, :].bitcast(I32), in_=x_scales[:, 4 * q : 4 * q + 4, :].bitcast(I32))
         load_context(0, 0)
         load_words(1)
@@ -72,15 +72,31 @@ def tile_picked_zmos_soft_p_kernel(tc, x_words, x_scales, hT, gT, mix, offs, out
             dst = keep.tile([P, P, PACK], BF16, name="grouped%d%d%d" % (m, o, t), align_bytes=64)
             grouped[m, o, t] = dst
             dst_view = dst[:].rearrange("p (c i) j -> p c j i", i=4)
-            src_view = raw[m, o][:, :, t * P : (t + 1) * P].rearrange("p j (c i) -> p c j i", i=4)
+            src_view = raw[m, o][:, 0:PACK, t * P : (t + 1) * P].rearrange("p j (c i) -> p c j i", i=4)
             if on_vector:
                 nc.vector.tensor_copy(out=dst_view, in_=src_view)
             else:
                 nc.scalar.copy(out=dst_view, in_=src_view)
 
+        quantised = {}
+
+        def warm_tensor(o):
+            codes, scales = quantised[0, 0, 0]
+            spare = psum.tile([P, S], F32, name="spare%d" % o)
+            nc.tensor.matmul_mx(
+                out=spare[:],
+                lhsT=codes[:].bitcast(FP8X4),
+                lhsT_scale=scales[:],
+                rhs=picked[o][:].bitcast(FP8X4),
+                rhs_scale=picked_planes[4 * o : P, :],
+                start=True,
+                stop=True,
+            )
+
         def multiply(m, o, t):
             codes = keep.tile([P, P], U32, name="codes%d%d%d" % (m, o, t), align_bytes=64)
             scales = keep.tile([P, P], U8, name="scales%d%d%d" % (m, o, t), align_bytes=64)
+            quantised[m, o, t] = (codes, scales)
             nc.vector.quantize_mx(out=codes[:].bitcast(FP8X4), scales=scales[:], in_=grouped[m, o, t][:].rearrange("p c j -> p (c j)"))
             nc.tensor.matmul_mx(
                 out=banks[m, t][:],
@@ -102,12 +118,12 @@ def tile_picked_zmos_soft_p_kernel(tc, x_words, x_scales, hT, gT, mix, offs, out
 
         def exponentiate(m, t):
             if (m, t) == (0, 1):
-                neg_max = grouped[1, 1, 1][:].rearrange("p c j -> p (c j)").bitcast(F32)[:, 0:1]
+                neg_max = raw[1, 1][:, 0, P : P + 1]
             else:
                 neg_max = keep.tile([P, 1], F32, name="neg_max%d%d" % (m, t))[:]
             totals[m, t] = keep.tile([P, 1], F32, name="total%d%d" % (m, t))
             if (m, t) == (0, 0):
-                exps[m, t] = raw[1, 1][:, :, P : 2 * P]
+                exps[m, t] = raw[1, 1][:, 1 : PACK + 1, P : 2 * P]
             else:
                 exps[m, t] = runs(keep.tile([P, S], F32, name="exps%d%d" % (m, t))[:])
             nc.vector.tensor_reduce(out=neg_max, in_=banks[m, t][:], axis=AX.X, op=ALU.max, negate=True)

@@ -87,8 +87,8 @@ def tile_picked_zmos_soft_p_kernel(tc, x_words, x_scales, hT, gT, mix, offs, out
                 out=spare[:],
                 lhsT=codes[:].bitcast(FP8X4),
                 lhsT_scale=scales[:],
-                rhs=picked[o][:].bitcast(FP8X4),
-                rhs_scale=picked_planes[4 * o : P, :],
+                rhs=picked[0][:].bitcast(FP8X4),
+                rhs_scale=picked_planes[:],
                 start=True,
                 stop=True,
             )
@@ -159,6 +159,8 @@ def tile_picked_zmos_soft_p_kernel(tc, x_words, x_scales, hT, gT, mix, offs, out
             interleave(0, 0, t, False)
         for t in range(TILES):
             multiply(0, 0, t)
+        warm_tensor(0)
+        warm_tensor(1)
         gather_words(1)
         for m, o in ((0, 1), (1, 0), (1, 1)):
             for t in range(TILES):

@@ -29,10 +29,11 @@ def tile_picked_zmos_soft_p_kernel(tc, x_words, x_scales, hT, gT, mix, offs, out
         keep = ctx.enter_context(tc.tile_pool(name="keep", bufs=1))
         psum = ctx.enter_context(tc.psum_pool(name="psum", bufs=1))
 
+        groups = [(m, t) for m in range(2) for t in range(TILES)]
         offsets = keep.tile([P, S // 16], U16, name="offsets")
         words = [keep.tile([P, T], U32, name="words%d" % o, align_bytes=64) for o in range(PASSES)]
         planes = keep.tile([P, T], U8, name="planes", align_bytes=64)
-        raw = {(m, o): keep.tile([P, PACK + 1, J], F32, name="raw%d%d" % (m, o), align_bytes=64) for m in range(2) for o in range(PASSES)}
+        raw = {(m, o): keep.tile([P, PACK, J], F32, name="raw%d%d" % (m, o), align_bytes=64) for m in range(2) for o in range(PASSES)}
         weights = keep.tile([P, TILES, 2], F32, name="weights")
         warm_in = keep.tile([P, 1], F32, name="warm_in")
         warm_out = keep.tile([P, 1], F32, name="warm_out")
@@ -46,58 +47,41 @@ def tile_picked_zmos_soft_p_kernel(tc, x_words, x_scales, hT, gT, mix, offs, out
 
         def load_context(m, o):
             rows = (hT, gT)[m][o * K_PASS : (o + 1) * K_PASS, :]
-            nc.sync.dma_start(out=raw[m, o][:, 0:PACK, :], in_=rows.rearrange("(p j) c -> p j c", j=PACK))
+            nc.sync.dma_start(out=raw[m, o][:], in_=rows.rearrange("(p j) c -> p j c", j=PACK))
 
         load_words(0)
         nc.sync.dma_start(offsets[:], offs)
         for q in (0, 2, 1, 3):
             nc.sync.dma_start(out=planes[32 * q : 32 * q + 8, :].bitcast(I32), in_=x_scales[:, 4 * q : 4 * q + 4, :].bitcast(I32))
-        load_context(0, 0)
         load_words(1)
-        load_context(0, 1)
-        load_context(1, 0)
-        load_context(1, 1)
+        for m in range(2):
+            for o in range(PASSES):
+                load_context(m, o)
         nc.sync.dma_start(out=weights[:], in_=mix.rearrange("(t p) c -> p t c", p=P))
 
         picked_planes = keep.tile([P, S], U8, name="picked_planes", align_bytes=64)
         picked = [keep.tile([P, S], U32, name="picked%d" % o, align_bytes=64) for o in range(PASSES)]
-        banks = {(m, t): psum.tile([P, S], F32, name="bank%d%d" % (m, t)) for m in range(2) for t in range(TILES)}
+        banks = {(m, t): psum.tile([P, S], F32, name="bank%d%d" % (m, t)) for m, t in groups}
 
         def gather_words(o):
             nc.vector.tensor_copy(picked[o][:], words[o][:].indirect(offsets[:]))
 
         grouped = {}
 
-        def interleave(m, o, t, on_vector):
-            dst = keep.tile([P, P, PACK], BF16, name="grouped%d%d%d" % (m, o, t), align_bytes=64)
-            grouped[m, o, t] = dst
+        def interleave(m, t, o, on_vector):
+            dst = keep.tile([P, P, PACK], BF16, name="grouped%d%d%d" % (m, t, o), tag="grouped%d%d%d" % (m, t, o), align_bytes=64)
+            grouped[m, t, o] = dst
             dst_view = dst[:].rearrange("p (c i) j -> p c j i", i=4)
-            src_view = raw[m, o][:, 0:PACK, t * P : (t + 1) * P].rearrange("p j (c i) -> p c j i", i=4)
+            src_view = raw[m, o][:, :, t * P : (t + 1) * P].rearrange("p j (c i) -> p c j i", i=4)
             if on_vector:
                 nc.vector.tensor_copy(out=dst_view, in_=src_view)
             else:
                 nc.scalar.copy(out=dst_view, in_=src_view)
 
-        quantised = {}
-
-        def warm_tensor(o):
-            codes, scales = quantised[0, 0, 0]
-            spare = psum.tile([P, S], F32, name="spare%d" % o)
-            nc.tensor.matmul_mx(
-                out=spare[:],
-                lhsT=codes[:].bitcast(FP8X4),
-                lhsT_scale=scales[:],
-                rhs=picked[0][:].bitcast(FP8X4),
-                rhs_scale=picked_planes[:],
-                start=True,
-                stop=True,
-            )
-
-        def multiply(m, o, t):
-            codes = keep.tile([P, P], U32, name="codes%d%d%d" % (m, o, t), align_bytes=64)
-            scales = keep.tile([P, P], U8, name="scales%d%d%d" % (m, o, t), align_bytes=64)
-            quantised[m, o, t] = (codes, scales)
-            nc.vector.quantize_mx(out=codes[:].bitcast(FP8X4), scales=scales[:], in_=grouped[m, o, t][:].rearrange("p c j -> p (c j)"))
+        def multiply(m, t, o):
+            codes = keep.tile([P, P], U32, name="codes%d%d%d" % (m, t, o), align_bytes=64)
+            scales = keep.tile([P, P], U8, name="scales%d%d%d" % (m, t, o), align_bytes=64)
+            nc.vector.quantize_mx(out=codes[:].bitcast(FP8X4), scales=scales[:], in_=grouped[m, t, o][:].rearrange("p c j -> p (c j)"))
             nc.tensor.matmul_mx(
                 out=banks[m, t][:],
                 lhsT=codes[:].bitcast(FP8X4),
@@ -113,9 +97,6 @@ def tile_picked_zmos_soft_p_kernel(tc, x_words, x_scales, hT, gT, mix, offs, out
         totals = {}
         first = {}
 
-        def runs(ap):
-            return ap.rearrange("p (j c) -> p j c", j=PACK)
-
         def exponentiate(m, t):
             if (m, t) == (0, 1):
                 neg_max = raw[1, 1][:, 0, P : P + 1]
@@ -123,11 +104,11 @@ def tile_picked_zmos_soft_p_kernel(tc, x_words, x_scales, hT, gT, mix, offs, out
                 neg_max = keep.tile([P, 1], F32, name="neg_max%d%d" % (m, t))[:]
             totals[m, t] = keep.tile([P, 1], F32, name="total%d%d" % (m, t))
             if (m, t) == (0, 0):
-                exps[m, t] = raw[1, 1][:, 1 : PACK + 1, P : 2 * P]
+                exps[m, t] = keep.tile([P, S], F32, name="exps%d%d" % (m, t), tag="grouped110", align_bytes=64)
             else:
-                exps[m, t] = runs(keep.tile([P, S], F32, name="exps%d%d" % (m, t))[:])
+                exps[m, t] = keep.tile([P, S], F32, name="exps%d%d" % (m, t))
             nc.vector.tensor_reduce(out=neg_max, in_=banks[m, t][:], axis=AX.X, op=ALU.max, negate=True)
-            nc.scalar.activation(out=exps[m, t], in_=runs(banks[m, t][:]), func=ACT.Exp, bias=neg_max, scale=1.0, accum_out=totals[m, t][:])
+            nc.scalar.activation(out=exps[m, t][:], in_=banks[m, t][:], func=ACT.Exp, bias=neg_max, scale=1.0, accum_out=totals[m, t][:])
 
         def invert(m, t):
             inverse[m, t] = keep.tile([P, 1], F32, name="inverse%d%d" % (m, t))
@@ -136,7 +117,7 @@ def tile_picked_zmos_soft_p_kernel(tc, x_words, x_scales, hT, gT, mix, offs, out
         def weigh_first(t):
             invert(0, t)
             first[t] = keep.tile([P, S], F32, name="first%d" % t)
-            nc.vector.tensor_scalar(out=runs(first[t][:]), in0=exps[0, t], scalar1=inverse[0, t][:], scalar2=weights[:, t, 0:1], op0=ALU.mult, op1=ALU.mult)
+            nc.vector.tensor_scalar(out=first[t][:], in0=exps[0, t][:], scalar1=inverse[0, t][:], scalar2=weights[:, t, 0:1], op0=ALU.mult, op1=ALU.mult)
 
         factor = {}
 
@@ -149,28 +130,20 @@ def tile_picked_zmos_soft_p_kernel(tc, x_words, x_scales, hT, gT, mix, offs, out
             for u, queue in enumerate((nc.sync, nc.scalar)):
                 half = keep.tile([P, S // 2], F32, name="result%d%d" % (t, u))
                 cols = slice(u * S // 2, (u + 1) * S // 2)
-                second = exps[1, t].rearrange("p j c -> p (j c)")
-                nc.vector.scalar_tensor_tensor(out=half[:], in0=second[:, cols], scalar=factor[t][:], in1=first[t][:, cols], op0=ALU.mult, op1=ALU.add)
+                nc.vector.scalar_tensor_tensor(out=half[:], in0=exps[1, t][:, cols], scalar=factor[t][:], in1=first[t][:, cols], op0=ALU.mult, op1=ALU.add)
                 queue.dma_start(out=out[t * P : (t + 1) * P, cols], in_=half[:])
 
         gather_words(0)
         nc.vector.tensor_copy(picked_planes[:], planes[:].indirect(offsets[:]))
-        for t in range(TILES):
-            interleave(0, 0, t, False)
-        for t in range(TILES):
-            multiply(0, 0, t)
-        warm_tensor(0)
-        warm_tensor(1)
         gather_words(1)
-        for m, o in ((0, 1), (1, 0), (1, 1)):
-            for t in range(TILES):
-                interleave(m, o, t, t == 0)
-            for t in range(TILES):
-                multiply(m, o, t)
-        exponentiate(0, 0)
-        exponentiate(0, 1)
-        exponentiate(1, 0)
-        exponentiate(1, 1)
+        for m in range(2):
+            for o in range(PASSES):
+                for t in range(TILES):
+                    interleave(m, t, o, t == 0 and (m, o) != (1, 0))
+                for t in range(TILES):
+                    multiply(m, t, o)
+        for m, t in groups:
+            exponentiate(m, t)
         for t in range(TILES):
             weigh_second(t)
         for t in range(TILES):

@@ -21,6 +21,7 @@ PACK = 4
 K_PASS = P * PACK
 PASSES = K // K_PASS
 TILES = J // P
+HALF = S // 2
 
 
 def tile_picked_zmos_soft_p_kernel(tc, x_words, x_scales, hT, gT, mix, offs, out):
@@ -33,7 +34,6 @@ def tile_picked_zmos_soft_p_kernel(tc, x_words, x_scales, hT, gT, mix, offs, out
         offsets = keep.tile([P, S // 16], U16, name="offsets")
         words = [keep.tile([P, T], U32, name="words%d" % o, align_bytes=64) for o in range(PASSES)]
         planes = keep.tile([P, T], U8, name="planes", align_bytes=64)
-        raw = {(m, o): keep.tile([P, PACK, J], F32, name="raw%d%d" % (m, o), align_bytes=64) for m in range(2) for o in range(PASSES)}
         weights = keep.tile([P, TILES, 2], F32, name="weights")
         warm_in = keep.tile([P, 1], F32, name="warm_in")
         warm_out = keep.tile([P, 1], F32, name="warm_out")
@@ -42,49 +42,53 @@ def tile_picked_zmos_soft_p_kernel(tc, x_words, x_scales, hT, gT, mix, offs, out
         nc.vector.memset(warm_in[:], 0.0)
         nc.scalar.activation(out=warm_out[:], in_=warm_in[:], func=ACT.Exp)
 
+        raw = {}
+
         def load_words(o):
             nc.sync.dma_start(out=words[o][:].bitcast(I32), in_=x_words[o].rearrange("p n r -> p (n r)").bitcast(I32))
 
-        def load_context(m, o):
+        def load_context(m, o, j0, j1):
+            raw[m, o, j0] = keep.tile([P, j1 - j0, J], F32, name="raw%d%d%d" % (m, o, j0), align_bytes=64)
             rows = (hT, gT)[m][o * K_PASS : (o + 1) * K_PASS, :]
-            nc.sync.dma_start(out=raw[m, o][:], in_=rows.rearrange("(p j) c -> p j c", j=PACK))
+            nc.sync.dma_start(out=raw[m, o, j0][:], in_=rows.rearrange("(p j) c -> p j c", j=PACK)[:, j0:j1, :])
 
         load_words(0)
         nc.sync.dma_start(offsets[:], offs)
         for q in (0, 2, 1, 3):
             nc.sync.dma_start(out=planes[32 * q : 32 * q + 8, :].bitcast(I32), in_=x_scales[:, 4 * q : 4 * q + 4, :].bitcast(I32))
+        load_context(0, 0, 0, 4)
         load_words(1)
-        for m in range(2):
-            for o in range(PASSES):
-                load_context(m, o)
+        load_context(0, 1, 0, 4)
+        load_context(1, 0, 0, 4)
+        load_context(1, 1, 0, 4)
         nc.sync.dma_start(out=weights[:], in_=mix.rearrange("(t p) c -> p t c", p=P))
 
         picked_planes = keep.tile([P, S], U8, name="picked_planes", align_bytes=64)
         picked = [keep.tile([P, S], U32, name="picked%d" % o, align_bytes=64) for o in range(PASSES)]
         banks = {(m, t): psum.tile([P, S], F32, name="bank%d%d" % (m, t)) for m, t in groups}
+        grouped = {(m, t, o): keep.tile([P, P, PACK], BF16, name="grouped%d%d%d" % (m, t, o), tag="grouped%d%d%d" % (m, t, o), align_bytes=64) for m, t in groups for o in range(PASSES)}
+
+        made = {}
 
         def gather_words(o):
             nc.vector.tensor_copy(picked[o][:], words[o][:].indirect(offsets[:]))
 
-        grouped = {}
-
-        def interleave(m, t, o, on_vector):
-            dst = keep.tile([P, P, PACK], BF16, name="grouped%d%d%d" % (m, t, o), tag="grouped%d%d%d" % (m, t, o), align_bytes=64)
-            grouped[m, t, o] = dst
-            dst_view = dst[:].rearrange("p (c i) j -> p c j i", i=4)
-            src_view = raw[m, o][:, :, t * P : (t + 1) * P].rearrange("p j (c i) -> p c j i", i=4)
+        def interleave(m, t, o, j0, j1, on_vector, c0=0, c1=P):
+            dst_view = grouped[m, t, o][:, c0:c1, j0:j1].rearrange("p (c i) j -> p c j i", i=4)
+            src_view = raw[m, o, j0][:, :, t * P + c0 : t * P + c1].rearrange("p j (c i) -> p c j i", i=4)
             if on_vector:
                 nc.vector.tensor_copy(out=dst_view, in_=src_view)
             else:
                 nc.scalar.copy(out=dst_view, in_=src_view)
 
-        def multiply(m, t, o):
-            codes = keep.tile([P, P], U32, name="codes%d%d%d" % (m, t, o), align_bytes=64)
+        def multiply(m, t, o, dst=None):
+            codes = dst if dst is not None else keep.tile([P, P], U32, name="codes%d%d%d" % (m, t, o), align_bytes=64)[:]
             scales = keep.tile([P, P], U8, name="scales%d%d%d" % (m, t, o), align_bytes=64)
-            nc.vector.quantize_mx(out=codes[:].bitcast(FP8X4), scales=scales[:], in_=grouped[m, t, o][:].rearrange("p c j -> p (c j)"))
+            nc.vector.quantize_mx(out=codes.bitcast(FP8X4), scales=scales[:], in_=grouped[m, t, o][:].rearrange("p c j -> p (c j)"))
+            made[m, t, o] = (codes, scales)
             nc.tensor.matmul_mx(
                 out=banks[m, t][:],
-                lhsT=codes[:].bitcast(FP8X4),
+                lhsT=codes.bitcast(FP8X4),
                 lhsT_scale=scales[:],
                 rhs=picked[o][:].bitcast(FP8X4),
                 rhs_scale=picked_planes[4 * o : P, :],
@@ -92,61 +96,77 @@ def tile_picked_zmos_soft_p_kernel(tc, x_words, x_scales, hT, gT, mix, offs, out
                 stop=(o == PASSES - 1),
             )
 
+        neg_max = {}
         exps = {}
-        inverse = {}
         totals = {}
+        inverse = {}
+        factor = {}
         first = {}
 
-        def exponentiate(m, t):
-            if (m, t) == (0, 1):
-                neg_max = raw[1, 1][:, 0, P : P + 1]
-            else:
-                neg_max = keep.tile([P, 1], F32, name="neg_max%d%d" % (m, t))[:]
+        def maximum(m, t, dst=None):
+            neg_max[m, t] = dst if dst is not None else keep.tile([P, 1], F32, name="neg_max%d%d" % (m, t))[:]
+            nc.vector.tensor_reduce(out=neg_max[m, t], in_=banks[m, t][:], axis=AX.X, op=ALU.max, negate=True)
+
+        def exponentiate(m, t, tag=None):
             totals[m, t] = keep.tile([P, 1], F32, name="total%d%d" % (m, t))
-            if (m, t) == (0, 0):
-                exps[m, t] = keep.tile([P, S], F32, name="exps%d%d" % (m, t), tag="grouped110", align_bytes=64)
-            else:
-                exps[m, t] = keep.tile([P, S], F32, name="exps%d%d" % (m, t))
-            nc.vector.tensor_reduce(out=neg_max, in_=banks[m, t][:], axis=AX.X, op=ALU.max, negate=True)
-            nc.scalar.activation(out=exps[m, t][:], in_=banks[m, t][:], func=ACT.Exp, bias=neg_max, scale=1.0, accum_out=totals[m, t][:])
+            exps[m, t] = keep.tile([P, S], F32, name="exps%d%d" % (m, t), tag=tag or "exps%d%d" % (m, t), align_bytes=64)
+            nc.scalar.activation(out=exps[m, t][:], in_=banks[m, t][:], func=ACT.Exp, bias=neg_max[m, t], scale=1.0, accum_out=totals[m, t][:])
 
         def invert(m, t):
             inverse[m, t] = keep.tile([P, 1], F32, name="inverse%d%d" % (m, t))
             nc.vector.reciprocal(out=inverse[m, t][:], in_=totals[m, t][:])
 
-        def weigh_first(t):
-            invert(0, t)
-            first[t] = keep.tile([P, S], F32, name="first%d" % t)
-            nc.vector.tensor_scalar(out=first[t][:], in0=exps[0, t][:], scalar1=inverse[0, t][:], scalar2=weights[:, t, 0:1], op0=ALU.mult, op1=ALU.mult)
+        def make_factor(m, t):
+            factor[m, t] = keep.tile([P, 1], F32, name="factor%d%d" % (m, t))
+            nc.vector.tensor_tensor(out=factor[m, t][:], in0=inverse[m, t][:], in1=weights[:, t, m : m + 1], op=ALU.mult)
 
-        factor = {}
-
-        def weigh_second(t):
-            invert(1, t)
-            factor[t] = keep.tile([P, 1], F32, name="factor%d" % t)
-            nc.vector.tensor_tensor(out=factor[t][:], in0=inverse[1, t][:], in1=weights[:, t, 1:2], op=ALU.mult)
-
-        def finish(t):
-            for u, queue in enumerate((nc.sync, nc.scalar)):
-                half = keep.tile([P, S // 2], F32, name="result%d%d" % (t, u))
-                cols = slice(u * S // 2, (u + 1) * S // 2)
-                nc.vector.scalar_tensor_tensor(out=half[:], in0=exps[1, t][:, cols], scalar=factor[t][:], in1=first[t][:, cols], op0=ALU.mult, op1=ALU.add)
-                queue.dma_start(out=out[t * P : (t + 1) * P, cols], in_=half[:])
+        def combine(t, u, queue):
+            half = keep.tile([P, HALF], F32, name="result%d%d" % (t, u))
+            cols = slice(u * HALF, (u + 1) * HALF)
+            nc.vector.scalar_tensor_tensor(out=half[:], in0=exps[1, t][:, cols], scalar=factor[1, t][:], in1=first[t][:, cols], op0=ALU.mult, op1=ALU.add)
+            queue.dma_start(out=out[t * P : (t + 1) * P, cols], in_=half[:])
 
         gather_words(0)
         nc.vector.tensor_copy(picked_planes[:], planes[:].indirect(offsets[:]))
+        for t in range(TILES):
+            interleave(0, t, 0, 0, 4, False)
+        for t in range(TILES):
+            multiply(0, t, 0)
+        spare = psum.tile([32, P], F32, name="spare")
+        for rep in range(6):
+            codes, scales = made[0, rep % TILES, 0]
+            nc.tensor.matmul_mx(out=spare[:], lhsT=codes[:, 0:32].bitcast(FP8X4), lhsT_scale=scales[:, 0:32], rhs=codes.bitcast(FP8X4), rhs_scale=scales[:], start=True, stop=True)
         gather_words(1)
-        for m in range(2):
-            for o in range(PASSES):
-                for t in range(TILES):
-                    interleave(m, t, o, t == 0 and (m, o) != (1, 0))
-                for t in range(TILES):
-                    multiply(m, t, o)
-        for m, t in groups:
-            exponentiate(m, t)
+        interleave(0, 0, 1, 0, 4, True, 0, 88)
+        interleave(0, 0, 1, 0, 4, False, 88, P)
+        interleave(0, 1, 1, 0, 4, False)
         for t in range(TILES):
-            weigh_second(t)
+            multiply(0, t, 1)
         for t in range(TILES):
-            weigh_first(t)
+            interleave(1, t, 0, 0, 4, False)
+        maximum(0, 0)
         for t in range(TILES):
-            finish(t)
+            interleave(1, t, 1, 0, 4, t == 0)
+        for t in range(TILES):
+            multiply(1, t, 0)
+        for t in range(TILES):
+            multiply(1, t, 1)
+        exponentiate(0, 0, "grouped110")
+        maximum(0, 1, raw[1, 1, 0][:, 0, P : P + 1])
+        exponentiate(0, 1)
+        for t in range(TILES):
+            maximum(1, t)
+            exponentiate(1, t)
+        for m, t in groups[:3]:
+            invert(m, t)
+        first[0] = keep.tile([P, S], F32, name="first0")
+        nc.vector.tensor_scalar(out=first[0][:], in0=exps[0, 0][:], scalar1=inverse[0, 0][:], scalar2=weights[:, 0, 0:1], op0=ALU.mult, op1=ALU.mult)
+        make_factor(1, 0)
+        first[1] = keep.tile([P, S], F32, name="first1")
+        nc.vector.tensor_scalar(out=first[1][:], in0=exps[0, 1][:], scalar1=inverse[0, 1][:], scalar2=weights[:, 1, 0:1], op0=ALU.mult, op1=ALU.mult)
+        invert(1, 1)
+        combine(0, 0, nc.sync)
+        make_factor(1, 1)
+        combine(0, 1, nc.scalar)
+        combine(1, 0, nc.sync)
+        combine(1, 1, nc.scalar)

@@ -21,7 +21,6 @@ PACK = 4
 K_PASS = P * PACK
 PASSES = K // K_PASS
 TILES = J // P
-HALF = S // 2
 
 
 def tile_picked_zmos_soft_p_kernel(tc, x_words, x_scales, hT, gT, mix, offs, out):
@@ -34,6 +33,7 @@ def tile_picked_zmos_soft_p_kernel(tc, x_words, x_scales, hT, gT, mix, offs, out
         offsets = keep.tile([P, S // 16], U16, name="offsets")
         words = [keep.tile([P, T], U32, name="words%d" % o, align_bytes=64) for o in range(PASSES)]
         planes = keep.tile([P, T], U8, name="planes", align_bytes=64)
+        raw = {(m, o): keep.tile([P, PACK, J], F32, name="raw%d%d" % (m, o), align_bytes=64) for m in range(2) for o in range(PASSES)}
         weights = keep.tile([P, TILES, 2], F32, name="weights")
         warm_in = keep.tile([P, 1], F32, name="warm_in")
         warm_out = keep.tile([P, 1], F32, name="warm_out")
@@ -42,53 +42,51 @@ def tile_picked_zmos_soft_p_kernel(tc, x_words, x_scales, hT, gT, mix, offs, out
         nc.vector.memset(warm_in[:], 0.0)
         nc.scalar.activation(out=warm_out[:], in_=warm_in[:], func=ACT.Exp)
 
-        raw = {}
-
         def load_words(o):
             nc.sync.dma_start(out=words[o][:].bitcast(I32), in_=x_words[o].rearrange("p n r -> p (n r)").bitcast(I32))
 
-        def load_context(m, o, j0, j1):
-            raw[m, o, j0] = keep.tile([P, j1 - j0, J], F32, name="raw%d%d%d" % (m, o, j0), align_bytes=64)
+        def load_context(m, o):
             rows = (hT, gT)[m][o * K_PASS : (o + 1) * K_PASS, :]
-            nc.sync.dma_start(out=raw[m, o, j0][:], in_=rows.rearrange("(p j) c -> p j c", j=PACK)[:, j0:j1, :])
+            nc.sync.dma_start(out=raw[m, o][:], in_=rows.rearrange("(p j) c -> p j c", j=PACK))
 
         load_words(0)
         nc.sync.dma_start(offsets[:], offs)
         for q in (0, 2, 1, 3):
             nc.sync.dma_start(out=planes[32 * q : 32 * q + 8, :].bitcast(I32), in_=x_scales[:, 4 * q : 4 * q + 4, :].bitcast(I32))
-        load_context(0, 0, 0, 4)
+        load_context(0, 0)
         load_words(1)
-        load_context(0, 1, 0, 4)
-        load_context(1, 0, 0, 4)
-        load_context(1, 1, 0, 4)
+        load_context(0, 1)
+        for o in range(PASSES):
+            load_context(1, o)
         nc.sync.dma_start(out=weights[:], in_=mix.rearrange("(t p) c -> p t c", p=P))
 
         picked_planes = keep.tile([P, S], U8, name="picked_planes", align_bytes=64)
         picked = [keep.tile([P, S], U32, name="picked%d" % o, align_bytes=64) for o in range(PASSES)]
         banks = {(m, t): psum.tile([P, S], F32, name="bank%d%d" % (m, t)) for m, t in groups}
-        grouped = {(m, t, o): keep.tile([P, P, PACK], BF16, name="grouped%d%d%d" % (m, t, o), tag="grouped%d%d%d" % (m, t, o), align_bytes=64) for m, t in groups for o in range(PASSES)}
-
-        made = {}
 
         def gather_words(o):
             nc.vector.tensor_copy(picked[o][:], words[o][:].indirect(offsets[:]))
 
-        def interleave(m, t, o, j0, j1, on_vector, c0=0, c1=P):
-            dst_view = grouped[m, t, o][:, c0:c1, j0:j1].rearrange("p (c i) j -> p c j i", i=4)
-            src_view = raw[m, o, j0][:, :, t * P + c0 : t * P + c1].rearrange("p j (c i) -> p c j i", i=4)
-            if on_vector:
-                nc.vector.tensor_copy(out=dst_view, in_=src_view)
-            else:
-                nc.scalar.copy(out=dst_view, in_=src_view)
+        grouped = {}
+        made = {}
 
-        def multiply(m, t, o, dst=None):
-            codes = dst if dst is not None else keep.tile([P, P], U32, name="codes%d%d%d" % (m, t, o), align_bytes=64)[:]
+        def interleave(m, t, o, vector_columns):
+            dst = keep.tile([P, P, PACK], BF16, name="grouped%d%d%d" % (m, t, o), tag="grouped%d%d%d" % (m, t, o), align_bytes=64)
+            grouped[m, t, o] = dst
+            for c0, c1, move in ((0, vector_columns, nc.vector.tensor_copy), (vector_columns, P, nc.scalar.copy)):
+                if c1 > c0:
+                    dst_view = dst[:, c0:c1, :].rearrange("p (c i) j -> p c j i", i=4)
+                    src_view = raw[m, o][:, :, t * P + c0 : t * P + c1].rearrange("p j (c i) -> p c j i", i=4)
+                    move(out=dst_view, in_=src_view)
+
+        def multiply(m, t, o):
+            codes = keep.tile([P, P], U32, name="codes%d%d%d" % (m, t, o), align_bytes=64)
             scales = keep.tile([P, P], U8, name="scales%d%d%d" % (m, t, o), align_bytes=64)
-            nc.vector.quantize_mx(out=codes.bitcast(FP8X4), scales=scales[:], in_=grouped[m, t, o][:].rearrange("p c j -> p (c j)"))
+            nc.vector.quantize_mx(out=codes[:].bitcast(FP8X4), scales=scales[:], in_=grouped[m, t, o][:].rearrange("p c j -> p (c j)"))
             made[m, t, o] = (codes, scales)
             nc.tensor.matmul_mx(
                 out=banks[m, t][:],
-                lhsT=codes.bitcast(FP8X4),
+                lhsT=codes[:].bitcast(FP8X4),
                 lhsT_scale=scales[:],
                 rhs=picked[o][:].bitcast(FP8X4),
                 rhs_scale=picked_planes[4 * o : P, :],
@@ -96,77 +94,67 @@ def tile_picked_zmos_soft_p_kernel(tc, x_words, x_scales, hT, gT, mix, offs, out
                 stop=(o == PASSES - 1),
             )
 
-        neg_max = {}
         exps = {}
-        totals = {}
         inverse = {}
-        factor = {}
+        totals = {}
         first = {}
 
-        def maximum(m, t, dst=None):
-            neg_max[m, t] = dst if dst is not None else keep.tile([P, 1], F32, name="neg_max%d%d" % (m, t))[:]
-            nc.vector.tensor_reduce(out=neg_max[m, t], in_=banks[m, t][:], axis=AX.X, op=ALU.max, negate=True)
-
-        def exponentiate(m, t, tag=None):
+        def exponentiate(m, t):
+            if (m, t) == (0, 1):
+                neg_max = raw[1, 1][:, 0, P : P + 1]
+            else:
+                neg_max = keep.tile([P, 1], F32, name="neg_max%d%d" % (m, t))[:]
             totals[m, t] = keep.tile([P, 1], F32, name="total%d%d" % (m, t))
-            exps[m, t] = keep.tile([P, S], F32, name="exps%d%d" % (m, t), tag=tag or "exps%d%d" % (m, t), align_bytes=64)
-            nc.scalar.activation(out=exps[m, t][:], in_=banks[m, t][:], func=ACT.Exp, bias=neg_max[m, t], scale=1.0, accum_out=totals[m, t][:])
+            if (m, t) == (0, 0):
+                exps[m, t] = keep.tile([P, S], F32, name="exps%d%d" % (m, t), tag="grouped110", align_bytes=64)
+            else:
+                exps[m, t] = keep.tile([P, S], F32, name="exps%d%d" % (m, t))
+            nc.vector.tensor_reduce(out=neg_max, in_=banks[m, t][:], axis=AX.X, op=ALU.max, negate=True)
+            nc.scalar.activation(out=exps[m, t][:], in_=banks[m, t][:], func=ACT.Exp, bias=neg_max, scale=1.0, accum_out=totals[m, t][:])
 
         def invert(m, t):
             inverse[m, t] = keep.tile([P, 1], F32, name="inverse%d%d" % (m, t))
             nc.vector.reciprocal(out=inverse[m, t][:], in_=totals[m, t][:])
 
-        def make_factor(m, t):
-            factor[m, t] = keep.tile([P, 1], F32, name="factor%d%d" % (m, t))
-            nc.vector.tensor_tensor(out=factor[m, t][:], in0=inverse[m, t][:], in1=weights[:, t, m : m + 1], op=ALU.mult)
+        def weigh_first(t):
+            invert(0, t)
+            first[t] = keep.tile([P, S], F32, name="first%d" % t)
+            nc.vector.tensor_scalar(out=first[t][:], in0=exps[0, t][:], scalar1=inverse[0, t][:], scalar2=weights[:, t, 0:1], op0=ALU.mult, op1=ALU.mult)
 
-        def combine(t, u, queue):
-            half = keep.tile([P, HALF], F32, name="result%d%d" % (t, u))
-            cols = slice(u * HALF, (u + 1) * HALF)
-            nc.vector.scalar_tensor_tensor(out=half[:], in0=exps[1, t][:, cols], scalar=factor[1, t][:], in1=first[t][:, cols], op0=ALU.mult, op1=ALU.add)
-            queue.dma_start(out=out[t * P : (t + 1) * P, cols], in_=half[:])
+        factor = {}
+
+        def weigh_second(t):
+            invert(1, t)
+            factor[t] = keep.tile([P, 1], F32, name="factor%d" % t)
+            nc.vector.tensor_tensor(out=factor[t][:], in0=inverse[1, t][:], in1=weights[:, t, 1:2], op=ALU.mult)
+
+        def finish(t):
+            for u, queue in enumerate((nc.sync, nc.scalar)):
+                half = keep.tile([P, S // 2], F32, name="result%d%d" % (t, u))
+                cols = slice(u * S // 2, (u + 1) * S // 2)
+                nc.vector.scalar_tensor_tensor(out=half[:], in0=exps[1, t][:, cols], scalar=factor[t][:], in1=first[t][:, cols], op0=ALU.mult, op1=ALU.add)
+                queue.dma_start(out=out[t * P : (t + 1) * P, cols], in_=half[:])
 
         gather_words(0)
         nc.vector.tensor_copy(picked_planes[:], planes[:].indirect(offsets[:]))
+        vector_share = {(0, 0): 0, (0, 1): 88, (1, 0): 0, (1, 1): P}
+        for m in range(2):
+            for o in range(PASSES):
+                for t in range(TILES):
+                    interleave(m, t, o, vector_share[m, o] if t == 0 else 0)
+                for t in range(TILES):
+                    multiply(m, t, o)
+                if (m, o) == (0, 0):
+                    spare = psum.tile([32, P], F32, name="spare")
+                    for rep in range(6):
+                        codes, scales = made[0, rep % TILES, 0]
+                        nc.tensor.matmul_mx(out=spare[:], lhsT=codes[:, 0:32].bitcast(FP8X4), lhsT_scale=scales[:, 0:32], rhs=codes[:].bitcast(FP8X4), rhs_scale=scales[:], start=True, stop=True)
+                    gather_words(1)
+        for m, t in groups:
+            exponentiate(m, t)
         for t in range(TILES):
-            interleave(0, t, 0, 0, 4, False)
+            weigh_second(t)
         for t in range(TILES):
-            multiply(0, t, 0)
-        spare = psum.tile([32, P], F32, name="spare")
-        for rep in range(6):
-            codes, scales = made[0, rep % TILES, 0]
-            nc.tensor.matmul_mx(out=spare[:], lhsT=codes[:, 0:32].bitcast(FP8X4), lhsT_scale=scales[:, 0:32], rhs=codes.bitcast(FP8X4), rhs_scale=scales[:], start=True, stop=True)
-        gather_words(1)
-        interleave(0, 0, 1, 0, 4, True, 0, 88)
-        interleave(0, 0, 1, 0, 4, False, 88, P)
-        interleave(0, 1, 1, 0, 4, False)
+            weigh_first(t)
         for t in range(TILES):
-            multiply(0, t, 1)
-        for t in range(TILES):
-            interleave(1, t, 0, 0, 4, False)
-        maximum(0, 0)
-        for t in range(TILES):
-            interleave(1, t, 1, 0, 4, t == 0)
-        for t in range(TILES):
-            multiply(1, t, 0)
-        for t in range(TILES):
-            multiply(1, t, 1)
-        exponentiate(0, 0, "grouped110")
-        maximum(0, 1, raw[1, 1, 0][:, 0, P : P + 1])
-        exponentiate(0, 1)
-        for t in range(TILES):
-            maximum(1, t)
-            exponentiate(1, t)
-        for m, t in groups[:3]:
-            invert(m, t)
-        first[0] = keep.tile([P, S], F32, name="first0")
-        nc.vector.tensor_scalar(out=first[0][:], in0=exps[0, 0][:], scalar1=inverse[0, 0][:], scalar2=weights[:, 0, 0:1], op0=ALU.mult, op1=ALU.mult)
-        make_factor(1, 0)
-        first[1] = keep.tile([P, S], F32, name="first1")
-        nc.vector.tensor_scalar(out=first[1][:], in0=exps[0, 1][:], scalar1=inverse[0, 1][:], scalar2=weights[:, 1, 0:1], op0=ALU.mult, op1=ALU.mult)
-        invert(1, 1)
-        combine(0, 0, nc.sync)
-        make_factor(1, 1)
-        combine(0, 1, nc.scalar)
-        combine(1, 0, nc.sync)
-        combine(1, 1, nc.scalar)
+            finish(t)

@@ -72,17 +72,23 @@ def tile_picked_zmos_soft_p_kernel(tc, x_words, x_scales, hT, gT, mix, offs, out
 
         def interleave(m, t, o, vector_columns):
             dst = keep.tile([P, P, PACK], BF16, name="grouped%d%d%d" % (m, t, o), tag="grouped%d%d%d" % (m, t, o), align_bytes=64)
-            grouped[m, t, o] = dst
+            grouped[m, t, o] = dst[:]
             for c0, c1, move in ((0, vector_columns, nc.vector.tensor_copy), (vector_columns, P, nc.scalar.copy)):
                 if c1 > c0:
                     dst_view = dst[:, c0:c1, :].rearrange("p (c i) j -> p c j i", i=4)
                     src_view = raw[m, o][:, :, t * P + c0 : t * P + c1].rearrange("p j (c i) -> p c j i", i=4)
                     move(out=dst_view, in_=src_view)
 
-        def multiply(m, t, o):
+        def interleave_both(m, o):
+            dst = keep.tile([P, J, PACK], BF16, name="grouped%d%d" % (m, o), align_bytes=64)
+            nc.scalar.copy(out=dst[:].rearrange("p (c i) j -> p c j i", i=4), in_=raw[m, o][:].rearrange("p j (c i) -> p c j i", i=4))
+            for t in range(TILES):
+                grouped[m, t, o] = dst[:, t * P : (t + 1) * P, :]
+
+        def multiply(m, t, o, opens):
             codes = keep.tile([P, P], U32, name="codes%d%d%d" % (m, t, o), align_bytes=64)
             scales = keep.tile([P, P], U8, name="scales%d%d%d" % (m, t, o), align_bytes=64)
-            nc.vector.quantize_mx(out=codes[:].bitcast(FP8X4), scales=scales[:], in_=grouped[m, t, o][:].rearrange("p c j -> p (c j)"))
+            nc.vector.quantize_mx(out=codes[:].bitcast(FP8X4), scales=scales[:], in_=grouped[m, t, o].rearrange("p c j -> p (c j)"))
             made[m, t, o] = (codes, scales)
             nc.tensor.matmul_mx(
                 out=banks[m, t][:],
@@ -90,8 +96,8 @@ def tile_picked_zmos_soft_p_kernel(tc, x_words, x_scales, hT, gT, mix, offs, out
                 lhsT_scale=scales[:],
                 rhs=picked[o][:].bitcast(FP8X4),
                 rhs_scale=picked_planes[4 * o : P, :],
-                start=(o == 0),
-                stop=(o == PASSES - 1),
+                start=opens,
+                stop=not opens,
             )
 
         exps = {}
@@ -106,7 +112,7 @@ def tile_picked_zmos_soft_p_kernel(tc, x_words, x_scales, hT, gT, mix, offs, out
                 neg_max = keep.tile([P, 1], F32, name="neg_max%d%d" % (m, t))[:]
             totals[m, t] = keep.tile([P, 1], F32, name="total%d%d" % (m, t))
             if (m, t) == (0, 0):
-                exps[m, t] = keep.tile([P, S], F32, name="exps%d%d" % (m, t), tag="grouped110", align_bytes=64)
+                exps[m, t] = keep.tile([P, S], F32, name="exps%d%d" % (m, t), tag="grouped101", align_bytes=64)
             else:
                 exps[m, t] = keep.tile([P, S], F32, name="exps%d%d" % (m, t))
             nc.vector.tensor_reduce(out=neg_max, in_=banks[m, t][:], axis=AX.X, op=ALU.max, negate=True)
@@ -137,19 +143,26 @@ def tile_picked_zmos_soft_p_kernel(tc, x_words, x_scales, hT, gT, mix, offs, out
 
         gather_words(0)
         nc.vector.tensor_copy(picked_planes[:], planes[:].indirect(offsets[:]))
-        vector_share = {(0, 0): 0, (0, 1): 88, (1, 0): 0, (1, 1): P}
-        for m in range(2):
-            for o in range(PASSES):
-                for t in range(TILES):
-                    interleave(m, t, o, vector_share[m, o] if t == 0 else 0)
-                for t in range(TILES):
-                    multiply(m, t, o)
-                if (m, o) == (0, 0):
-                    spare = psum.tile([32, P], F32, name="spare")
-                    for rep in range(6):
-                        codes, scales = made[0, rep % TILES, 0]
-                        nc.tensor.matmul_mx(out=spare[:], lhsT=codes[:, 0:32].bitcast(FP8X4), lhsT_scale=scales[:, 0:32], rhs=codes[:].bitcast(FP8X4), rhs_scale=scales[:], start=True, stop=True)
-                    gather_words(1)
+        for t in range(TILES):
+            interleave(0, t, 0, 0)
+        for t in range(TILES):
+            multiply(0, t, 0, True)
+        spare = psum.tile([32, P], F32, name="spare")
+        for rep in range(6):
+            codes, scales = made[0, rep % TILES, 0]
+            nc.tensor.matmul_mx(out=spare[:], lhsT=codes[:, 0:32].bitcast(FP8X4), lhsT_scale=scales[:, 0:32], rhs=codes[:].bitcast(FP8X4), rhs_scale=scales[:], start=True, stop=True)
+        gather_words(1)
+        for t in range(TILES):
+            interleave(0, t, 1, 64 if t == 0 else 0)
+        for t in range(TILES):
+            multiply(0, t, 1, False)
+        interleave_both(1, 0)
+        for t in range(TILES):
+            interleave(1, t, 1, P if t == 0 else 0)
+        multiply(1, 0, 0, True)
+        multiply(1, 0, 1, False)
+        multiply(1, 1, 1, True)
+        multiply(1, 1, 0, False)
         for m, t in groups:
             exponentiate(m, t)
         for t in range(TILES):

@@ -21,6 +21,7 @@ PACK = 4
 K_PASS = P * PACK
 PASSES = K // K_PASS
 TILES = J // P
+BURST = 256
 
 
 def tile_picked_zmos_soft_p_kernel(tc, x_words, x_scales, hT, gT, mix, offs, out):
@@ -31,9 +32,9 @@ def tile_picked_zmos_soft_p_kernel(tc, x_words, x_scales, hT, gT, mix, offs, out
 
         groups = [(m, t) for m in range(2) for t in range(TILES)]
         offsets = keep.tile([P, S // 16], U16, name="offsets")
-        words = [keep.tile([P, T], U32, name="words%d" % o, align_bytes=64) for o in range(PASSES)]
-        planes = keep.tile([P, T], U8, name="planes", align_bytes=64)
-        raw = {(m, o): keep.tile([P, PACK, J], F32, name="raw%d%d" % (m, o), align_bytes=64) for m in range(2) for o in range(PASSES)}
+        words = [keep.tile([P, T], U32, name="words%d" % o, align_bytes=BURST) for o in range(PASSES)]
+        planes = keep.tile([P, T], U8, name="planes", align_bytes=BURST)
+        raw = {(m, o): keep.tile([P, PACK, J], F32, name="raw%d%d" % (m, o), align_bytes=BURST) for m in range(2) for o in range(PASSES)}
         weights = keep.tile([P, TILES, 2], F32, name="weights")
         warm_in = keep.tile([P, 1], F32, name="warm_in")
         warm_out = keep.tile([P, 1], F32, name="warm_out")
@@ -108,6 +109,8 @@ def tile_picked_zmos_soft_p_kernel(tc, x_words, x_scales, hT, gT, mix, offs, out
         def exponentiate(m, t):
             if (m, t) == (0, 1):
                 neg_max = raw[1, 1][:, 0, P : P + 1]
+            elif (m, t) == (1, 1):
+                neg_max = keep.tile([P, 1], F32, name="neg_max11", tag="result0", align_bytes=BURST)[:]
             else:
                 neg_max = keep.tile([P, 1], F32, name="neg_max%d%d" % (m, t))[:]
             totals[m, t] = keep.tile([P, 1], F32, name="total%d%d" % (m, t))
@@ -125,7 +128,14 @@ def tile_picked_zmos_soft_p_kernel(tc, x_words, x_scales, hT, gT, mix, offs, out
         def weigh_first(t):
             invert(0, t)
             first[t] = keep.tile([P, S], F32, name="first%d" % t)
-            nc.vector.tensor_scalar(out=first[t][:], in0=exps[0, t][:], scalar1=inverse[0, t][:], scalar2=weights[:, t, 0:1], op0=ALU.mult, op1=ALU.mult)
+            if t == 0:
+                nc.vector.tensor_scalar(out=first[t][:], in0=exps[0, t][:], scalar1=inverse[0, t][:], scalar2=weights[:, t, 0:1], op0=ALU.mult, op1=ALU.mult)
+            else:
+                share = keep.tile([P, 1], F32, name="share")
+                nc.vector.tensor_tensor(out=share[:], in0=inverse[0, t][:], in1=weights[:, t, 0:1], op=ALU.mult)
+                for u in range(2):
+                    cols = slice(u * S // 2, (u + 1) * S // 2)
+                    nc.scalar.activation(out=first[t][:, cols], in_=exps[0, t][:, cols], func=ACT.Copy, scale=share[:])
 
         factor = {}
 
@@ -135,11 +145,11 @@ def tile_picked_zmos_soft_p_kernel(tc, x_words, x_scales, hT, gT, mix, offs, out
             nc.vector.tensor_tensor(out=factor[t][:], in0=inverse[1, t][:], in1=weights[:, t, 1:2], op=ALU.mult)
 
         def finish(t):
-            for u, queue in enumerate((nc.sync, nc.scalar)):
-                half = keep.tile([P, S // 2], F32, name="result%d%d" % (t, u))
+            result = keep.tile([P, S], F32, name="result%d" % t, tag="result%d" % t, align_bytes=BURST)
+            for u, queue in enumerate((nc.sync, nc.scalar if t else nc.sync)):
                 cols = slice(u * S // 2, (u + 1) * S // 2)
-                nc.vector.scalar_tensor_tensor(out=half[:], in0=exps[1, t][:, cols], scalar=factor[t][:], in1=first[t][:, cols], op0=ALU.mult, op1=ALU.add)
-                queue.dma_start(out=out[t * P : (t + 1) * P, cols], in_=half[:])
+                nc.vector.scalar_tensor_tensor(out=result[:, cols], in0=exps[1, t][:, cols], scalar=factor[t][:], in1=first[t][:, cols], op0=ALU.mult, op1=ALU.add)
+                queue.dma_start(out=out[t * P : (t + 1) * P, cols], in_=result[:, cols])
 
         gather_words(0)
         nc.vector.tensor_copy(picked_planes[:], planes[:].indirect(offsets[:]))
@@ -167,7 +177,7 @@ def tile_picked_zmos_soft_p_kernel(tc, x_words, x_scales, hT, gT, mix, offs, out
             exponentiate(m, t)
         for t in range(TILES):
             weigh_second(t)
-        for t in range(TILES):
+        for t in (1, 0):
             weigh_first(t)
         for t in range(TILES):
             finish(t)

@@ -146,7 +146,7 @@ def tile_picked_zmos_soft_p_kernel(tc, x_words, x_scales, hT, gT, mix, offs, out
 
         def finish(t):
             result = keep.tile([P, S], F32, name="result%d" % t, tag="result%d" % t, align_bytes=BURST)
-            for u, queue in enumerate((nc.sync, nc.scalar if t else nc.sync)):
+            for u, queue in enumerate((nc.sync, nc.scalar)):
                 cols = slice(u * S // 2, (u + 1) * S // 2)
                 nc.vector.scalar_tensor_tensor(out=result[:, cols], in0=exps[1, t][:, cols], scalar=factor[t][:], in1=first[t][:, cols], op0=ALU.mult, op1=ALU.add)
                 queue.dma_start(out=out[t * P : (t + 1) * P, cols], in_=result[:, cols])

@@ -146,7 +146,7 @@ def tile_picked_zmos_soft_p_kernel(tc, x_words, x_scales, hT, gT, mix, offs, out
 
         def finish(t):
             result = keep.tile([P, S], F32, name="result%d" % t, tag="result%d" % t, align_bytes=BURST)
-            for u, queue in enumerate((nc.sync, nc.scalar)):
+            for u, queue in enumerate((nc.scalar, nc.sync)):
                 cols = slice(u * S // 2, (u + 1) * S // 2)
                 nc.vector.scalar_tensor_tensor(out=result[:, cols], in0=exps[1, t][:, cols], scalar=factor[t][:], in1=first[t][:, cols], op0=ALU.mult, op1=ALU.add)
                 queue.dma_start(out=out[t * P : (t + 1) * P, cols], in_=result[:, cols])

from contextlib import ExitStack

import concourse.mybir as mybir

K, T, S, J = 1024, 2048, 512, 256
FLOPS = 2 * 2 * K * J * S

F32 = mybir.dt.float32
BF16 = mybir.dt.bfloat16
I32 = mybir.dt.int32
U32 = mybir.dt.uint32
U16 = mybir.dt.uint16
U8 = mybir.dt.uint8
FP8X4 = mybir.dt.float8_e4m3fn_x4
ALU = mybir.AluOpType
ACT = mybir.ActivationFunctionType
AX = mybir.AxisListType

P = 128
PACK = 4
K_PASS = P * PACK
PASSES = K // K_PASS
TILES = J // P
BURST = 256


def tile_picked_zmos_soft_p_kernel(tc, x_words, x_scales, hT, gT, mix, offs, out):
    nc = tc.nc
    with ExitStack() as ctx:
        keep = ctx.enter_context(tc.tile_pool(name="keep", bufs=1))
        psum = ctx.enter_context(tc.psum_pool(name="psum", bufs=1))

        groups = [(m, t) for m in range(2) for t in range(TILES)]
        offsets = keep.tile([P, S // 16], U16, name="offsets")
        words = [keep.tile([P, T], U32, name="words%d" % o, align_bytes=BURST) for o in range(PASSES)]
        planes = keep.tile([P, T], U8, name="planes", align_bytes=BURST)
        raw = {(m, o): keep.tile([P, PACK, J], F32, name="raw%d%d" % (m, o), align_bytes=BURST) for m in range(2) for o in range(PASSES)}
        weights = keep.tile([P, TILES, 2], F32, name="weights")
        warm_in = keep.tile([P, 1], F32, name="warm_in")
        warm_out = keep.tile([P, 1], F32, name="warm_out")

        nc.vector.memset(planes[:].bitcast(I32), 0)
        nc.vector.memset(warm_in[:], 0.0)
        nc.scalar.activation(out=warm_out[:], in_=warm_in[:], func=ACT.Exp)

        def load_words(o):
            nc.sync.dma_start(out=words[o][:].bitcast(I32), in_=x_words[o].rearrange("p n r -> p (n r)").bitcast(I32))

        def load_context(m, o):
            rows = (hT, gT)[m][o * K_PASS : (o + 1) * K_PASS, :]
            nc.sync.dma_start(out=raw[m, o][:], in_=rows.rearrange("(p j) c -> p j c", j=PACK))

        load_words(0)
        nc.sync.dma_start(offsets[:], offs)
        for q in (0, 2, 1, 3):
            nc.sync.dma_start(out=planes[32 * q : 32 * q + 8, :].bitcast(I32), in_=x_scales[:, 4 * q : 4 * q + 4, :].bitcast(I32))
        load_context(0, 0)
        load_words(1)
        load_context(0, 1)
        for o in range(PASSES):
            load_context(1, o)
        nc.sync.dma_start(out=weights[:], in_=mix.rearrange("(t p) c -> p t c", p=P))

        picked_planes = keep.tile([P, S], U8, name="picked_planes", align_bytes=64)
        picked = [keep.tile([P, S], U32, name="picked%d" % o, align_bytes=64) for o in range(PASSES)]
        banks = {(m, t): psum.tile([P, S], F32, name="bank%d%d" % (m, t)) for m, t in groups}

        def gather_words(o):
            nc.vector.tensor_copy(picked[o][:], words[o][:].indirect(offsets[:]))

        grouped = {}
        made = {}

        def interleave(m, t, o, vector_columns):
            dst = keep.tile([P, P, PACK], BF16, name="grouped%d%d%d" % (m, t, o), tag="grouped%d%d%d" % (m, t, o), align_bytes=64)
            grouped[m, t, o] = dst[:]
            for c0, c1, move in ((0, vector_columns, nc.vector.tensor_copy), (vector_columns, P, nc.scalar.copy)):
                if c1 > c0:
                    dst_view = dst[:, c0:c1, :].rearrange("p (c i) j -> p c j i", i=4)
                    src_view = raw[m, o][:, :, t * P + c0 : t * P + c1].rearrange("p j (c i) -> p c j i", i=4)
                    move(out=dst_view, in_=src_view)

        def interleave_both(m, o):
            dst = keep.tile([P, J, PACK], BF16, name="grouped%d%d" % (m, o), align_bytes=64)
            nc.scalar.copy(out=dst[:].rearrange("p (c i) j -> p c j i", i=4), in_=raw[m, o][:].rearrange("p j (c i) -> p c j i", i=4))
            for t in range(TILES):
                grouped[m, t, o] = dst[:, t * P : (t + 1) * P, :]

        def multiply(m, t, o, opens):
            codes = keep.tile([P, P], U32, name="codes%d%d%d" % (m, t, o), align_bytes=64)
            scales = keep.tile([P, P], U8, name="scales%d%d%d" % (m, t, o), align_bytes=64)
            nc.vector.quantize_mx(out=codes[:].bitcast(FP8X4), scales=scales[:], in_=grouped[m, t, o].rearrange("p c j -> p (c j)"))
            made[m, t, o] = (codes, scales)
            nc.tensor.matmul_mx(
                out=banks[m, t][:],
                lhsT=codes[:].bitcast(FP8X4),
                lhsT_scale=scales[:],
                rhs=picked[o][:].bitcast(FP8X4),
                rhs_scale=picked_planes[4 * o : P, :],
                start=opens,
                stop=not opens,
            )

        exps = {}
        inverse = {}
        totals = {}
        first = {}

        def exponentiate(m, t):
            if (m, t) == (0, 1):
                neg_max = raw[1, 1][:, 0, P : P + 1]
            elif (m, t) == (1, 1):
                neg_max = keep.tile([P, 1], F32, name="neg_max11", tag="result0", align_bytes=BURST)[:]
            else:
                neg_max = keep.tile([P, 1], F32, name="neg_max%d%d" % (m, t))[:]
            totals[m, t] = keep.tile([P, 1], F32, name="total%d%d" % (m, t))
            if (m, t) == (0, 0):
                exps[m, t] = keep.tile([P, S], F32, name="exps%d%d" % (m, t), tag="grouped101", align_bytes=64)
            else:
                exps[m, t] = keep.tile([P, S], F32, name="exps%d%d" % (m, t))
            nc.vector.tensor_reduce(out=neg_max, in_=banks[m, t][:], axis=AX.X, op=ALU.max, negate=True)
            nc.scalar.activation(out=exps[m, t][:], in_=banks[m, t][:], func=ACT.Exp, bias=neg_max, scale=1.0, accum_out=totals[m, t][:])

        def invert(m, t):
            inverse[m, t] = keep.tile([P, 1], F32, name="inverse%d%d" % (m, t))
            nc.vector.reciprocal(out=inverse[m, t][:], in_=totals[m, t][:])

        def weigh_first(t):
            invert(0, t)
            first[t] = keep.tile([P, S], F32, name="first%d" % t)
            if t == 0:
                nc.vector.tensor_scalar(out=first[t][:], in0=exps[0, t][:], scalar1=inverse[0, t][:], scalar2=weights[:, t, 0:1], op0=ALU.mult, op1=ALU.mult)
            else:
                share = keep.tile([P, 1], F32, name="share")
                nc.vector.tensor_tensor(out=share[:], in0=inverse[0, t][:], in1=weights[:, t, 0:1], op=ALU.mult)
                for u in range(2):
                    cols = slice(u * S // 2, (u + 1) * S // 2)
                    nc.scalar.activation(out=first[t][:, cols], in_=exps[0, t][:, cols], func=ACT.Copy, scale=share[:])

        factor = {}

        def weigh_second(t):
            invert(1, t)
            factor[t] = keep.tile([P, 1], F32, name="factor%d" % t)
            nc.vector.tensor_tensor(out=factor[t][:], in0=inverse[1, t][:], in1=weights[:, t, 1:2], op=ALU.mult)

        def finish(t):
            result = keep.tile([P, S], F32, name="result%d" % t, tag="result%d" % t, align_bytes=BURST)
            for u, queue in enumerate((nc.scalar, nc.sync)):
                cols = slice(u * S // 2, (u + 1) * S // 2)
                nc.vector.scalar_tensor_tensor(out=result[:, cols], in0=exps[1, t][:, cols], scalar=factor[t][:], in1=first[t][:, cols], op0=ALU.mult, op1=ALU.add)
                queue.dma_start(out=out[t * P : (t + 1) * P, cols], in_=result[:, cols])

        gather_words(0)
        nc.vector.tensor_copy(picked_planes[:], planes[:].indirect(offsets[:]))
        for t in range(TILES):
            interleave(0, t, 0, 0)
        for t in range(TILES):
            multiply(0, t, 0, True)
        spare = psum.tile([32, P], F32, name="spare")
        for rep in range(6):
            codes, scales = made[0, rep % TILES, 0]
            nc.tensor.matmul_mx(out=spare[:], lhsT=codes[:, 0:32].bitcast(FP8X4), lhsT_scale=scales[:, 0:32], rhs=codes[:].bitcast(FP8X4), rhs_scale=scales[:], start=True, stop=True)
        gather_words(1)
        for t in range(TILES):
            interleave(0, t, 1, 64 if t == 0 else 0)
        for t in range(TILES):
            multiply(0, t, 1, False)
        interleave_both(1, 0)
        for t in range(TILES):
            interleave(1, t, 1, P if t == 0 else 0)
        multiply(1, 0, 0, True)
        multiply(1, 0, 1, False)
        multiply(1, 1, 1, True)
        multiply(1, 1, 0, False)
        for m, t in groups:
            exponentiate(m, t)
        for t in range(TILES):
            weigh_second(t)
        for t in (1, 0):
            weigh_first(t)
        for t in range(TILES):
            finish(t)
